import numpy as np
import ml_dtypes


def mxq(x, axis, fmt="e4m3"):
    dtype, down = {"e4m3": (ml_dtypes.float8_e4m3fn, 7), "e5m2": (ml_dtypes.float8_e5m2, 14)}[fmt]
    v = np.moveaxis(np.asarray(x, np.float32).astype(ml_dtypes.bfloat16).astype(np.float64), axis, -1)
    blocks = v.reshape(v.shape[:-1] + (-1, 32))
    amax = np.abs(blocks).max(-1, keepdims=True)
    byte = np.maximum(np.where(amax > 0, np.frexp(amax)[1] - 1 + 127, 0) - down, 1)
    scale = np.exp2(byte - 127.0)
    codes = (blocks / scale).astype(np.float32).astype(dtype).astype(np.float64)
    return np.moveaxis((codes * scale).reshape(v.shape), -1, axis)


WIDE = False


def mx_kscale(k):
    if not WIDE:
        return np.ones(k)
    levels = np.array([10, -10, 5, -5, 0])
    if k % 512:
        return np.exp2(np.random.permutation(np.resize(levels, k // 32))).repeat(32)
    a = np.empty((k // 512, 16))
    for p in range(k // 512):
        a[p, :8] = np.random.permutation(np.resize(levels, 8))
        for g in range(8):
            far = levels[np.abs(levels - a[p, g]) >= 10]
            a[p, g + 8] = far[np.random.randint(len(far))]
    return np.exp2(a.ravel()).repeat(32)


def f64(x):
    return np.asarray(x).astype(np.float64)


def striped(idx):
    return np.tile(np.asarray(idx).reshape(-1, 16).T, (8, 1)).astype(np.uint16)


def unstriped(offs):
    return offs[:16].T.reshape(-1).astype(np.int64)


E2M1 = np.array([0.0, 0.5, 1.0, 1.5, 2.0, 3.0, 4.0, 6.0, -0.0, -0.5, -1.0, -1.5, -2.0, -3.0, -4.0, -6.0])


def pack_weight(w, fmt):
    k, n = w.shape
    w = f64(np.asarray(w, np.float32).astype(ml_dtypes.bfloat16)).reshape(k // 32, 32, n)
    amax = np.abs(w).max(1)
    if fmt == "e4m3":
        byte = np.frexp(amax)[1] - 1 + 127 - 7
    else:
        mant, ex = np.frexp(amax / 6.0)
        byte = np.where(mant > 0.5, ex, ex - 1) + 127
    byte = np.clip(np.where(amax > 0, byte, 1), 1, 254)
    scaled = (w * np.exp2(127.0 - byte)[:, None, :]).reshape(k, n).astype(np.float32)
    by_word = np.ascontiguousarray(scaled.reshape(k // 512, 128, 4, n).transpose(0, 1, 3, 2))
    if fmt == "e4m3":
        words = by_word.astype(ml_dtypes.float8_e4m3fn).view(np.uint8)
    else:
        c = by_word.astype(ml_dtypes.float4_e2m1fn).view(np.uint8) & 0xF
        words = (c[..., 0::2] | (c[..., 1::2] << 4)).reshape(k // 512, 128, 2 * n)
    return np.ascontiguousarray(words), np.ascontiguousarray(byte.astype(np.uint8).reshape(k // 512, 16, n))


def unpack_weight(words, scales, fmt):
    g, _, n = scales.shape
    words = np.ascontiguousarray(words).reshape(g, 128, n, -1)
    if fmt == "e4m3":
        vals = words.view(ml_dtypes.float8_e4m3fn).astype(np.float64)
    else:
        nib = np.empty((g, 128, n, 4), np.uint8)
        nib[..., 0::2] = words & 0xF
        nib[..., 1::2] = words >> 4
        vals = E2M1[nib]
    vals = vals * np.repeat(np.exp2(scales.astype(np.float64) - 127.0), 8, axis=1)[..., None]
    return vals.transpose(0, 1, 3, 2).reshape(g * 512, n)


B, N, T, D, DV, NQ = 2, 512, 2048, 1024, 128, 128
CAP = 2.0


def setup_inputs():
    n = np.random.standard_normal
    seg = T // B
    idx = np.concatenate([b * seg + np.random.permutation(seg)[:N] for b in range(B)])
    s = mx_kscale(D)[:, None]
    u = np.ones(T)
    u[idx] = mx_kscale(B * N)
    r = np.random.uniform(0.5, 2.0, T)
    qp = [pack_weight(x, "e4m3") for x in n((B, D, NQ)) * s * (0.80 / np.sqrt(D))]
    k = n((D, T)) / s
    v = n((DV, T)) / (u * r)
    kp = pack_weight(k, "e2m1")
    return {
        "q_words": np.stack([x[0] for x in qp]),
        "q_scales": np.stack([x[1] for x in qp]),
        "k_words": np.ascontiguousarray(kp[0].reshape(D // 1024, 2, 128, T, 2).transpose(0, 2, 3, 1, 4)).reshape(D // 1024, 128, T, 4),
        "k_scales": kp[1],
        "vT": v.astype(np.float32),
        "vs": np.tile(u * r, (128, 1)).astype(np.float32),
        "kb": np.tile(n(T), (128, 1)).astype(np.float32),
        "offs": striped(idx),
    }


def reference(q_words, q_scales, k_words, k_scales, vT, vs, kb, offs):
    idx = unstriped(offs)
    k = unpack_weight(k_words.reshape(D // 1024, 128, T, 2, 2).transpose(0, 3, 1, 2, 4).reshape(D // 512, 128, 2 * T), k_scales, "e2m1")
    v = f64(vT)
    pick = lambda x: x[:, idx].reshape(x.shape[0], B, N).transpose(1, 0, 2)
    q = np.stack([unpack_weight(q_words[b], q_scales[b], "e4m3") for b in range(B)])
    score = q.transpose(0, 2, 1) @ pick(k)
    score = score + pick(f64(kb))[:, :1, :]
    score = CAP * np.tanh(score / CAP)
    p = 1.0 / (1.0 + np.exp(-score))
    w = p * pick(f64(vs))[:, :1, :]
    y = mxq(w, 2, "e4m3") @ mxq(pick(v).transpose(0, 2, 1), 1, "e4m3")
    y = y / 16.0
    return y

@@ -1,0 +1,204 @@
+from contextlib import ExitStack
+
+import concourse.mybir as mybir
+from concourse.masks import make_identity
+
+B, N, T, D, DV, NQ = 2, 512, 2048, 1024, 128, 128
+P = 128
+PACK = 4
+PASSES = D // (P * PACK)
+SEG = T // B
+COLS = N // 16
+CAP = 2.0
+
+FLOPS = 2 * B * NQ * N * (D + DV)
+
+F32 = mybir.dt.float32
+BF16 = mybir.dt.bfloat16
+I32 = mybir.dt.int32
+U32 = mybir.dt.uint32
+U16 = mybir.dt.uint16
+U8 = mybir.dt.uint8
+FP8X4 = mybir.dt.float8_e4m3fn_x4
+FP4X4 = mybir.dt.float4_e2m1fn_x4
+ACT = mybir.ActivationFunctionType
+ALU = mybir.AluOpType
+
+
+def tile_attend_sigm_cap_kb_segb2q128n512t2048_kernel(tc, q_words, q_scales, k_words, k_scales, vT, vs, kb, offs, out):
+    nc = tc.nc
+    with ExitStack() as ctx:
+        sb = ctx.enter_context(tc.tile_pool(name="sb", bufs=1))
+        ps = ctx.enter_context(tc.psum_pool(name="ps", bufs=1))
+
+        offsets = sb.tile([P, B * COLS], U16, name="offsets")
+        nc.sync.dma_start(offsets[:], offs)
+
+        def listed(window, b):
+            return window.indirect(offsets[:, b * COLS : (b + 1) * COLS])
+
+        ks_pool = sb.tile([P, T], U8, name="ks_pool", align_bytes=64)
+        nc.sync.dma_start(ks_pool[0:32, :].bitcast(I32), k_scales.bitcast(I32).rearrange("o f t -> (o f) t"))
+        nc.vector.memset(ks_pool[32:64, :].bitcast(I32), 0)
+        nc.vector.memset(ks_pool[64:128, :].bitcast(I32), 0)
+
+        kb_pool = sb.tile([P, T], F32, name="kb_pool", align_bytes=64)
+        nc.vector.memset(kb_pool[:].bitcast(I32), 0)
+
+        kw_pool = sb.tile([P, T], I32, name="kw_pool", align_bytes=64)
+        kw_dram = k_words[0].rearrange("g t x -> g (t x)").bitcast(I32)
+        v_raw = [
+            sb.tile([P, SEG], F32, name="v_raw0", tag="reused", align_bytes=64),
+            sb.tile([P, SEG], F32, name="v_raw1", align_bytes=64),
+        ]
+        qw = sb.tile([P, B * PASSES, NQ], I32, name="qw", align_bytes=64)
+        nc.sync.dma_start(kw_pool[:, 0:SEG], kw_dram[:, 0:SEG])
+        nc.sync.dma_start(v_raw[0][:], vT[:, 0:SEG])
+        nc.sync.dma_start(kw_pool[:, SEG:T], kw_dram[:, SEG:T])
+        nc.sync.dma_start(v_raw[1][:], vT[:, SEG:T])
+        nc.sync.dma_start(qw[:], q_words.rearrange("b o g q r -> g (b o) (q r)").bitcast(I32))
+        nc.sync.dma_start(kb_pool[0:1, :], kb[0:1, :])
+
+        ident = sb.tile([P, P], F32, name="ident", align_bytes=64)
+        make_identity(nc, ident[:])
+        qs = sb.tile([P, B * PASSES * NQ], U8, name="qs", align_bytes=64)
+        nc.gpsimd.memset(qs[:].bitcast(I32), 0)
+        qs_rows = q_scales.bitcast(I32).rearrange("b o (h r) q -> r h (b o) q", r=4)
+        for r in range(4):
+            nc.sync.dma_start(qs[r:P:32, :].bitcast(I32).rearrange("h (c q) -> h c q", c=B * PASSES), qs_rows[r])
+        ks1 = sb.tile([P, B * N], U8, name="ks1", align_bytes=64)
+        nc.gpsimd.memset(ks1[:].bitcast(I32), 0)
+
+        warm = sb.tile([P, 1], F32, name="warm")
+        nc.scalar.activation(warm[:], ident[:, 0:1], ACT.Sigmoid)
+
+        ks_got = sb.tile([P, B * N], U8, name="ks_got", align_bytes=64)
+        nc.vector.tensor_copy(ks_got[:], ks_pool[:].indirect(offsets[:]))
+        ks0 = sb.tile([P, B * N], U8, name="ks0", align_bytes=64)
+        ks_planes = [ks0, ks1]
+
+        def deal_key_scales():
+            nc.vector.tensor_copy(
+                ks0[:].rearrange("p (b t s) -> p b t s", b=B, t=PACK),
+                ks_got[:].rearrange("p (b s t) -> p b t s", b=B, t=PACK),
+            )
+            for o in range(PASSES):
+                for h in range(4):
+                    if (o, h) != (0, 0):
+                        row = 16 * o + 4 * h
+                        nc.sync.dma_start(ks_planes[o][32 * h : 32 * h + 4, :].bitcast(I32), ks0[row : row + 4, :].bitcast(I32))
+
+        v_pool = sb.tile([P, T], BF16, name="v_pool", align_bytes=64)
+
+        def row_to_columns(row, name):
+            cols = sb.tile([P, PACK], F32, name=name)
+            nc.sync.dma_start(cols[:], row[0:1, :].rearrange("o (s t) -> o s t", t=PACK))
+            return cols
+
+        def keys(b):
+            got = sb.tile([P, N], U32, name=f"kw_got{b}", align_bytes=64)
+            nc.vector.tensor_copy(got[:], listed(kw_pool[:, 0 : (b + 1) * SEG].bitcast(U32), b))
+            return got
+
+        def part(got, b):
+            parted = sb.tile([P, PASSES * N * 2], U8, name=f"kw_part{b}", align_bytes=64)
+            nc.vector.tensor_copy(
+                parted[:].bitcast(U16).rearrange("p (o t c i) -> p o c t i", o=PASSES, t=PACK, i=4),
+                got[:].bitcast(U16).rearrange("p (c i t o) -> p o c t i", o=PASSES, t=PACK, i=4),
+            )
+            return parted
+
+        def half_bias(b):
+            got = sb.tile([P, N], F32, name=f"kb_got{b}", align_bytes=64)
+            nc.vector.tensor_copy(got[:], listed(kb_pool[:], b))
+            cols = row_to_columns(got, f"kb_cols{b}")
+            half = sb.tile([P, PACK], F32, name=f"kb_half{b}")
+            nc.scalar.activation(half[:], cols[:], ACT.Copy, scale=1.0 / CAP)
+            return half
+
+        def token_scale(b):
+            got = sb.tile([P, N], F32, name=f"vs_got{b}", align_bytes=64)
+            nc.vector.tensor_copy(got[:], listed(vs_pool[:], b))
+            return row_to_columns(got, f"vs_cols{b}")
+
+        def values(b):
+            nc.scalar.copy(v_pool[:, b * SEG : (b + 1) * SEG], v_raw[b][:])
+            got = sb.tile([P, N], BF16, name=f"v_got{b}", align_bytes=64)
+            nc.scalar.activation(
+                got[:].rearrange("p (u s e) -> p s u e", u=2, e=2),
+                listed(v_pool[:, 0 : (b + 1) * SEG], b),
+                ACT.Copy,
+            )
+            turned = ps.tile([P, 2, P], F32, name=f"v_turn{b}")
+            for u in range(2):
+                nc.tensor.transpose(turned[:, u, :], got[:].bitcast(F32)[:, u * P : (u + 1) * P], ident[:])
+            nc.scalar.copy(woven[:, b, :].bitcast(F32).rearrange("p (e u) -> p e u", u=2), turned[:].rearrange("p u e -> p e u"))
+
+        def weights(b, parted, bias):
+            scores = ps.tile([P, PACK, NQ], F32, name=f"scores{b}")
+            for t in range(PACK):
+                for o in range(PASSES):
+                    c = b * PASSES + o
+                    nc.tensor.matmul_mx(
+                        scores[:, t, :],
+                        lhsT=parted[:, (o * PACK + t) * 2 * P : (o * PACK + t + 1) * 2 * P].bitcast(FP4X4),
+                        lhsT_scale=ks_planes[o][:, b * N + t * P : b * N + (t + 1) * P],
+                        rhs=qw[:, c, :].bitcast(FP8X4),
+                        rhs_scale=qs[:, c * NQ : (c + 1) * NQ],
+                        start=(o == 0),
+                        stop=(o == PASSES - 1),
+                    )
+            capped = sb.tile([P, PACK, NQ], F32, name=f"capped{b}", align_bytes=64)
+            for t in range(PACK):
+                nc.scalar.activation(capped[:, t, :], scores[:, t, :], ACT.Tanh, bias=bias[:, t : t + 1], scale=1.0 / CAP)
+            prob = sb.tile([P, NQ, PACK], F32, name=f"prob{b}", align_bytes=64)
+            nc.scalar.activation(prob[:], capped[:].rearrange("p t q -> p q t"), ACT.Sigmoid, scale=CAP)
+            return prob
+
+        def quantise(src, name):
+            codes = sb.tile([P, P], U32, name=name + "_codes", align_bytes=64)
+            scales = sb.tile([P, P], U8, name=name + "_scales", align_bytes=64)
+            nc.vector.quantize_mx(codes[:].bitcast(FP8X4), scales[:], src)
+            return codes, scales
+
+        woven = sb.tile([P, B, DV * PACK], BF16, name="woven", align_bytes=64)
+        got0 = keys(0)
+        deal_key_scales()
+        got1 = keys(1)
+        parted0 = part(got0, 0)
+        parted1 = part(got1, 1)
+        values(0)
+        vs_pool = sb.tile([P, T], F32, name="vs_pool", tag="reused", align_bytes=64)
+        nc.sync.dma_start(vs_pool[:], vs)
+        values(1)
+        bias0 = half_bias(0)
+        bias1 = half_bias(1)
+        prob0 = weights(0, parted0, bias0)
+        prob1 = weights(1, parted1, bias1)
+        scale0 = token_scale(0)
+        scale1 = token_scale(1)
+        v_codes = sb.tile([P, B * DV], U32, name="v_codes", tag="reused", align_bytes=64)
+        v_scales = sb.tile([P, B * DV], U8, name="v_scales", align_bytes=64)
+        nc.vector.quantize_mx(v_codes[:].bitcast(FP8X4), v_scales[:], woven[:].rearrange("p b x -> p (b x)"))
+        wq = []
+        w_bf = []
+        for b, (prob, scale) in enumerate(((prob0, scale0), (prob1, scale1))):
+            w = sb.tile([P, NQ, PACK], BF16, name=f"w{b}", align_bytes=64)
+            nc.vector.tensor_tensor(w[:], prob[:], scale[:].unsqueeze(1).to_broadcast([P, NQ, PACK]), ALU.mult)
+            w_bf.append(w)
+        for b in range(B):
+            wq.append(quantise(w_bf[b][:].rearrange("p q t -> p (q t)"), f"wq{b}"))
+        for b in range(B):
+            y = ps.tile([P, DV], F32, name=f"y{b}")
+            nc.tensor.matmul_mx(
+                y[:],
+                lhsT=wq[b][0][:].bitcast(FP8X4),
+                lhsT_scale=wq[b][1][:],
+                rhs=v_codes[:, b * DV : (b + 1) * DV].bitcast(FP8X4),
+                rhs_scale=v_scales[:, b * DV : (b + 1) * DV],
+                start=True,
+                stop=True,
+            )
+            res = sb.tile([P, DV], F32, name=f"res{b}")
+            nc.scalar.activation(res[:], y[:], ACT.Copy, scale=1.0 / 16.0)
+            nc.sync.dma_start(out[b], res[:])

@@ -10,6 +10,7 @@ PASSES = D // (P * PACK)
 SEG = T // B
 COLS = N // 16
 CAP = 2.0
+RUN = 4
 
 FLOPS = 2 * B * NQ * N * (D + DV)
 
@@ -29,118 +30,150 @@ def tile_attend_sigm_cap_kb_segb2q128n512t2048_kernel(tc, q_words, q_scales, k_w
     nc = tc.nc
     with ExitStack() as ctx:
         sb = ctx.enter_context(tc.tile_pool(name="sb", bufs=1))
+        al = ctx.enter_context(tc.tile_pool(name="al", bufs=1))
         ps = ctx.enter_context(tc.psum_pool(name="ps", bufs=1))
 
         offsets = sb.tile([P, B * COLS], U16, name="offsets")
         nc.sync.dma_start(offsets[:], offs)
 
+        def dealt(tile_ap):
+            return tile_ap.rearrange("p (t m i) -> p m t i", t=PACK, i=RUN)
+
         def listed(window, b):
             return window.indirect(offsets[:, b * COLS : (b + 1) * COLS])
 
-        ks_pool = sb.tile([P, T], U8, name="ks_pool", align_bytes=64)
+        warm_in = sb.tile([P, 1], F32, name="warm_in")
+        nc.vector.memset(warm_in[:], 0.0)
+        warm = sb.tile([P, 1], F32, name="warm")
+        nc.scalar.activation(warm[:], warm_in[:], ACT.Sigmoid)
+
+        ks_pool = al.tile([P, T], U8, name="ks_pool", offset=11264, align_bytes=64)
         nc.sync.dma_start(ks_pool[0:32, :].bitcast(I32), k_scales.bitcast(I32).rearrange("o f t -> (o f) t"))
-        nc.vector.memset(ks_pool[32:64, :].bitcast(I32), 0)
-        nc.vector.memset(ks_pool[64:128, :].bitcast(I32), 0)
-
-        kb_pool = sb.tile([P, T], F32, name="kb_pool", align_bytes=64)
-        nc.vector.memset(kb_pool[:].bitcast(I32), 0)
-
         kw_pool = sb.tile([P, T], I32, name="kw_pool", align_bytes=64)
         kw_dram = k_words[0].rearrange("g t x -> g (t x)").bitcast(I32)
-        v_raw = [
-            sb.tile([P, SEG], F32, name="v_raw0", tag="reused", align_bytes=64),
-            sb.tile([P, SEG], F32, name="v_raw1", align_bytes=64),
-        ]
-        qw = sb.tile([P, B * PASSES, NQ], I32, name="qw", align_bytes=64)
+        v_raw = [sb.tile([P, SEG], F32, name=f"v_raw{b}", align_bytes=64) for b in range(B)]
+        for h in range(2):
+            nc.sync.dma_start(v_raw[0][:, h * SEG // 2 : (h + 1) * SEG // 2], vT[:, h * SEG // 2 : (h + 1) * SEG // 2])
         nc.sync.dma_start(kw_pool[:, 0:SEG], kw_dram[:, 0:SEG])
-        nc.sync.dma_start(v_raw[0][:], vT[:, 0:SEG])
-        nc.sync.dma_start(kw_pool[:, SEG:T], kw_dram[:, SEG:T])
         nc.sync.dma_start(v_raw[1][:], vT[:, SEG:T])
-        nc.sync.dma_start(qw[:], q_words.rearrange("b o g q r -> g (b o) (q r)").bitcast(I32))
-        nc.sync.dma_start(kb_pool[0:1, :], kb[0:1, :])
+        nc.sync.dma_start(kw_pool[:, SEG:T], kw_dram[:, SEG:T])
 
-        ident = sb.tile([P, P], F32, name="ident", align_bytes=64)
-        make_identity(nc, ident[:])
         qs = sb.tile([P, B * PASSES * NQ], U8, name="qs", align_bytes=64)
         nc.gpsimd.memset(qs[:].bitcast(I32), 0)
         qs_rows = q_scales.bitcast(I32).rearrange("b o (h r) q -> r h (b o) q", r=4)
         for r in range(4):
             nc.sync.dma_start(qs[r:P:32, :].bitcast(I32).rearrange("h (c q) -> h c q", c=B * PASSES), qs_rows[r])
+        nc.gpsimd.memset(ks_pool[32:64, :].bitcast(I32), 0)
+        nc.gpsimd.memset(ks_pool[64:128, :].bitcast(I32), 0)
+        kb_pool = al.tile([P, T], F32, name="kb_pool", offset=0, align_bytes=64)
+        nc.gpsimd.memset(kb_pool[:].bitcast(I32), 0)
+        nc.scalar.dma_start(kb_pool[0:1, :], kb[0:1, :])
+        ident_bf = sb.tile([P, P], BF16, name="ident_bf", align_bytes=64)
+        ident = sb.tile([P, P], F32, name="ident", align_bytes=64)
         ks1 = sb.tile([P, B * N], U8, name="ks1", align_bytes=64)
         nc.gpsimd.memset(ks1[:].bitcast(I32), 0)
-
-        warm = sb.tile([P, 1], F32, name="warm")
-        nc.scalar.activation(warm[:], ident[:, 0:1], ACT.Sigmoid)
+        make_identity(nc, ident_bf[:])
+        make_identity(nc, ident[:])
+        vs_pool = al.tile([P, T], F32, name="vs_pool", offset=16384, align_bytes=64)
+        nc.gpsimd.memset(vs_pool[:].bitcast(I32), 0)
 
         ks_got = sb.tile([P, B * N], U8, name="ks_got", align_bytes=64)
-        nc.vector.tensor_copy(ks_got[:], ks_pool[:].indirect(offsets[:]))
+        for b in range(B):
+            nc.vector.tensor_copy(ks_got[:, b * N : (b + 1) * N], listed(ks_pool[:], b))
+        qw = al.tile([P, B * PASSES, NQ], I32, name="qw", offset=12288, align_bytes=64)
+        nc.sync.dma_start(qw[:], q_words.rearrange("b o g q r -> g (b o) (q r)").bitcast(I32))
         ks0 = sb.tile([P, B * N], U8, name="ks0", align_bytes=64)
         ks_planes = [ks0, ks1]
 
         def deal_key_scales():
-            nc.vector.tensor_copy(
-                ks0[:].rearrange("p (b t s) -> p b t s", b=B, t=PACK),
-                ks_got[:].rearrange("p (b s t) -> p b t s", b=B, t=PACK),
-            )
+            for b in range(B):
+                nc.vector.tensor_copy(
+                    ks0[:, b * N : (b + 1) * N].bitcast(I32).rearrange("p (t m) -> p t m", t=PACK),
+                    ks_got[:, b * N : (b + 1) * N].bitcast(I32).rearrange("p (m t) -> p t m", t=PACK),
+                )
             for o in range(PASSES):
                 for h in range(4):
                     if (o, h) != (0, 0):
                         row = 16 * o + 4 * h
                         nc.sync.dma_start(ks_planes[o][32 * h : 32 * h + 4, :].bitcast(I32), ks0[row : row + 4, :].bitcast(I32))
 
-        v_pool = sb.tile([P, T], BF16, name="v_pool", align_bytes=64)
+        v_pool = al.tile([P, T], BF16, name="v_pool", offset=28672, align_bytes=64)
 
-        def row_to_columns(row, name):
-            cols = sb.tile([P, PACK], F32, name=name)
-            nc.sync.dma_start(cols[:], row[0:1, :].rearrange("o (s t) -> o s t", t=PACK))
-            return cols
 
         def keys(b):
-            got = sb.tile([P, N], U32, name=f"kw_got{b}", align_bytes=64)
-            nc.vector.tensor_copy(got[:], listed(kw_pool[:, 0 : (b + 1) * SEG].bitcast(U32), b))
+            got = al.tile([P, N], U32, name=f"kw_got{b}", offset=(24576, 0)[b], align_bytes=64)
+            nc.vector.tensor_copy(dealt(got[:]), listed(kw_pool[:, 0 : (b + 1) * SEG].bitcast(U32), b))
             return got
 
         def part(got, b):
-            parted = sb.tile([P, PASSES * N * 2], U8, name=f"kw_part{b}", align_bytes=64)
+            parted = al.tile([P, PASSES * N * 2], U8, name=f"kw_part{b}", offset=(2048, 26624)[b], align_bytes=64)
             nc.vector.tensor_copy(
-                parted[:].bitcast(U16).rearrange("p (o t c i) -> p o c t i", o=PASSES, t=PACK, i=4),
-                got[:].bitcast(U16).rearrange("p (c i t o) -> p o c t i", o=PASSES, t=PACK, i=4),
+                parted[:].bitcast(U16).rearrange("p (o x) -> p o x", o=PASSES),
+                got[:].bitcast(U16).rearrange("p (x o) -> p o x", o=PASSES),
             )
             return parted
 
-        def half_bias(b):
-            got = sb.tile([P, N], F32, name=f"kb_got{b}", align_bytes=64)
-            nc.vector.tensor_copy(got[:], listed(kb_pool[:], b))
-            cols = row_to_columns(got, f"kb_cols{b}")
-            half = sb.tile([P, PACK], F32, name=f"kb_half{b}")
-            nc.scalar.activation(half[:], cols[:], ACT.Copy, scale=1.0 / CAP)
+        def gather_biases():
+            got = sb.tile([P, B * N], U32, name="kb_got", align_bytes=64)
+            nc.vector.tensor_copy(dealt(got[:]), kb_pool[:].bitcast(U32).indirect(offsets[:]))
+            return got
+
+        def half_bias(got, b):
+            turned = ps.tile([P, PACK, P], F32, name=f"kb_turn{b}", tag=f"turn{b}")
+            for t in range(PACK):
+                first = (t * B + b) * P
+                nc.tensor.transpose(turned[:, t, :], got[:, first : first + P].bitcast(F32), ident[:])
+            half = al.tile([P, PACK], F32, name=f"kb_half{b}", offset=30720 + 64 * b, align_bytes=64)
+            nc.scalar.activation(half[:], turned[:, :, 0], ACT.Copy, scale=1.0 / CAP)
             return half
 
         def token_scale(b):
-            got = sb.tile([P, N], F32, name=f"vs_got{b}", align_bytes=64)
-            nc.vector.tensor_copy(got[:], listed(vs_pool[:], b))
-            return row_to_columns(got, f"vs_cols{b}")
+            got = sb.tile([P, N], U32, name=f"vs_got{b}", align_bytes=64)
+            nc.vector.tensor_copy(dealt(got[:]), listed(vs_pool[:].bitcast(U32), b))
+            turned = ps.tile([P, PACK, P], F32, name=f"vs_turn{b}", tag=f"bank{b}_0")
+            for t in range(PACK):
+                nc.tensor.transpose(turned[:, t, :], got[:, t * P : (t + 1) * P].bitcast(F32), ident[:])
+            return turned[:, :, 0:1].rearrange("p t o -> p o t")
 
-        def values(b):
-            nc.scalar.copy(v_pool[:, b * SEG : (b + 1) * SEG], v_raw[b][:])
+        def values(b, pieces, scalar_cols):
+            width = SEG // pieces
+            for h in range(pieces):
+                nc.scalar.copy(v_pool[:, b * SEG + h * width : b * SEG + (h + 1) * width], v_raw[b][:, h * width : (h + 1) * width])
             got = sb.tile([P, N], BF16, name=f"v_got{b}", align_bytes=64)
+            first = b * COLS
             nc.scalar.activation(
-                got[:].rearrange("p (u s e) -> p s u e", u=2, e=2),
-                listed(v_pool[:, 0 : (b + 1) * SEG], b),
+                dealt(got[:])[:, 0:scalar_cols],
+                v_pool[:, 0 : (b + 1) * SEG].indirect(offsets[:, first : first + scalar_cols]),
                 ACT.Copy,
             )
-            turned = ps.tile([P, 2, P], F32, name=f"v_turn{b}")
-            for u in range(2):
-                nc.tensor.transpose(turned[:, u, :], got[:].bitcast(F32)[:, u * P : (u + 1) * P], ident[:])
-            nc.scalar.copy(woven[:, b, :].bitcast(F32).rearrange("p (e u) -> p e u", u=2), turned[:].rearrange("p u e -> p e u"))
+            if scalar_cols < COLS:
+                nc.vector.tensor_copy(
+                    dealt(got[:])[:, scalar_cols:COLS],
+                    v_raw[b][:].indirect(offsets[:, first + scalar_cols : first + COLS]),
+                )
+            return got
+
+        def turn_values(got, b, tags):
+            woven = al.tile([P, DV, PACK], BF16, name=f"v_woven{b}", offset=(31744, 18432)[b], align_bytes=64)
+            places = PACK // len(tags)
+            for h, tag in enumerate(tags):
+                turned = ps.tile([P, places, P], BF16, name=f"v_turn{b}_{h}", tag=tag)
+                for j in range(places):
+                    t = h * places + j
+                    nc.tensor.transpose(turned[:, j, :], got[:, t * P : (t + 1) * P], ident_bf[:])
+                (nc.scalar.copy, nc.vector.tensor_copy)[b](woven[:, :, h * places : (h + 1) * places], turned[:].rearrange("p t e -> p e t"))
+            return woven
 
         def weights(b, parted, bias):
-            scores = ps.tile([P, PACK, NQ], F32, name=f"scores{b}")
+            banks = [
+                ps.tile([P, 2, NQ], F32, name=f"scores{b}_{h}", tag=f"bank{b}_{h}") for h in range(2)
+            ]
+            scores = [banks[t // 2][:, t % 2, :] for t in range(PACK)]
             for t in range(PACK):
                 for o in range(PASSES):
                     c = b * PASSES + o
                     nc.tensor.matmul_mx(
-                        scores[:, t, :],
+                        scores[t],
                         lhsT=parted[:, (o * PACK + t) * 2 * P : (o * PACK + t + 1) * 2 * P].bitcast(FP4X4),
                         lhsT_scale=ks_planes[o][:, b * N + t * P : b * N + (t + 1) * P],
                         rhs=qw[:, c, :].bitcast(FP8X4),
@@ -148,9 +181,12 @@ def tile_attend_sigm_cap_kb_segb2q128n512t2048_kernel(tc, q_words, q_scales, k_w
                         start=(o == 0),
                         stop=(o == PASSES - 1),
                     )
-            capped = sb.tile([P, PACK, NQ], F32, name=f"capped{b}", align_bytes=64)
+            capped = al.tile([P, PACK, NQ], F32, name=f"capped{b}", offset=(28672, 32768)[b], align_bytes=64)
             for t in range(PACK):
-                nc.scalar.activation(capped[:, t, :], scores[:, t, :], ACT.Tanh, bias=bias[:, t : t + 1], scale=1.0 / CAP)
+                nc.scalar.activation(capped[:, t, :], scores[t], ACT.Tanh, bias=bias[:, t : t + 1], scale=1.0 / CAP)
+            return capped
+
+        def sigmoid(capped, b):
             prob = sb.tile([P, NQ, PACK], F32, name=f"prob{b}", align_bytes=64)
             nc.scalar.activation(prob[:], capped[:].rearrange("p t q -> p q t"), ACT.Sigmoid, scale=CAP)
             return prob
@@ -161,35 +197,41 @@ def tile_attend_sigm_cap_kb_segb2q128n512t2048_kernel(tc, q_words, q_scales, k_w
             nc.vector.quantize_mx(codes[:].bitcast(FP8X4), scales[:], src)
             return codes, scales
 
-        woven = sb.tile([P, B, DV * PACK], BF16, name="woven", align_bytes=64)
-        got0 = keys(0)
         deal_key_scales()
-        got1 = keys(1)
+        nc.sync.dma_start(vs_pool[0:1, :], vs[0:1, :])
+        v_got0 = values(0, 2, COLS)
+        v_got1 = values(1, 1, COLS)
+        got0 = keys(0)
+        kb_got = gather_biases()
         parted0 = part(got0, 0)
-        parted1 = part(got1, 1)
-        values(0)
-        vs_pool = sb.tile([P, T], F32, name="vs_pool", tag="reused", align_bytes=64)
-        nc.sync.dma_start(vs_pool[:], vs)
-        values(1)
-        bias0 = half_bias(0)
-        bias1 = half_bias(1)
-        prob0 = weights(0, parted0, bias0)
-        prob1 = weights(1, parted1, bias1)
+        parted1 = part(keys(1), 1)
+        v_codes = al.tile([P, B * DV], U32, name="v_codes", offset=16384, align_bytes=64)
+        v_scales = sb.tile([P, B * DV], U8, name="v_scales", align_bytes=64)
+
+        def quantise_values(woven, b):
+            cols = slice(b * DV, (b + 1) * DV)
+            nc.vector.quantize_mx(v_codes[:, cols].bitcast(FP8X4), v_scales[:, cols], woven[:].rearrange("p e t -> p (e t)"))
+
+        bias0 = half_bias(kb_got, 0)
+        bias1 = half_bias(kb_got, 1)
+        woven0 = turn_values(v_got0, 0, ("values0",))
+        prob0 = sigmoid(weights(0, parted0, bias0), 0)
+        prob1 = sigmoid(weights(1, parted1, bias1), 1)
         scale0 = token_scale(0)
         scale1 = token_scale(1)
-        v_codes = sb.tile([P, B * DV], U32, name="v_codes", tag="reused", align_bytes=64)
-        v_scales = sb.tile([P, B * DV], U8, name="v_scales", align_bytes=64)
-        nc.vector.quantize_mx(v_codes[:].bitcast(FP8X4), v_scales[:], woven[:].rearrange("p b x -> p (b x)"))
+        woven1 = turn_values(v_got1, 1, ("bank0_1",))
         wq = []
         w_bf = []
         for b, (prob, scale) in enumerate(((prob0, scale0), (prob1, scale1))):
             w = sb.tile([P, NQ, PACK], BF16, name=f"w{b}", align_bytes=64)
-            nc.vector.tensor_tensor(w[:], prob[:], scale[:].unsqueeze(1).to_broadcast([P, NQ, PACK]), ALU.mult)
+            nc.vector.tensor_tensor(w[:], prob[:], scale.to_broadcast([P, NQ, PACK]), ALU.mult)
             w_bf.append(w)
+        quantise_values(woven0, 0)
         for b in range(B):
             wq.append(quantise(w_bf[b][:].rearrange("p q t -> p (q t)"), f"wq{b}"))
+        quantise_values(woven1, 1)
         for b in range(B):
-            y = ps.tile([P, DV], F32, name=f"y{b}")
+            y = ps.tile([P, DV], F32, name=f"y{b}", tag=f"turn{b}")
             nc.tensor.matmul_mx(
                 y[:],
                 lhsT=wq[b][0][:].bitcast(FP8X4),

@@ -9,8 +9,10 @@ PACK = 4
 PASSES = D // (P * PACK)
 SEG = T // B
 COLS = N // 16
-CAP = 2.0
 RUN = 4
+QUAD = 32
+CAP = 2.0
+OUT_SCALE = 1.0 / 16.0
 
 FLOPS = 2 * B * NQ * N * (D + DV)
 
@@ -24,6 +26,19 @@ FP8X4 = mybir.dt.float8_e4m3fn_x4
 FP4X4 = mybir.dt.float4_e2m1fn_x4
 ACT = mybir.ActivationFunctionType
 ALU = mybir.AluOpType
+
+KIB = 1024
+AT_KB_POOL = 0
+AT_KW_GOT = (24 * KIB, AT_KB_POOL)
+AT_KW_PART = (AT_KB_POOL + 2 * KIB, 26 * KIB)
+AT_KS_POOL = 11 * KIB
+AT_QW = AT_KS_POOL + KIB
+AT_VS_POOL = 16 * KIB
+AT_KS_GOT = AT_VS_POOL
+AT_V_CODES = AT_VS_POOL
+AT_V_POOL = 28 * KIB
+AT_CAPPED = (AT_V_POOL, 32 * KIB)
+AT_WOVEN = (AT_V_POOL + 3 * KIB, AT_VS_POOL + 2 * KIB)
 
 
 def tile_attend_sigm_cap_kb_segb2q128n512t2048_kernel(tc, q_words, q_scales, k_words, k_scales, vT, vs, kb, offs, out):
@@ -47,8 +62,8 @@ def tile_attend_sigm_cap_kb_segb2q128n512t2048_kernel(tc, q_words, q_scales, k_w
         warm = sb.tile([P, 1], F32, name="warm")
         nc.scalar.activation(warm[:], warm_in[:], ACT.Sigmoid)
 
-        ks_pool = al.tile([P, T], U8, name="ks_pool", offset=11264, align_bytes=64)
-        nc.sync.dma_start(ks_pool[0:32, :].bitcast(I32), k_scales.bitcast(I32).rearrange("o f t -> (o f) t"))
+        ks_pool = al.tile([P, T], U8, name="ks_pool", offset=AT_KS_POOL, align_bytes=64)
+        nc.sync.dma_start(ks_pool[0:QUAD, :].bitcast(I32), k_scales.bitcast(I32).rearrange("o f t -> (o f) t"))
         kw_pool = sb.tile([P, T], I32, name="kw_pool", align_bytes=64)
         kw_dram = k_words[0].rearrange("g t x -> g (t x)").bitcast(I32)
         v_raw = [sb.tile([P, SEG], F32, name=f"v_raw{b}", align_bytes=64) for b in range(B)]
@@ -62,10 +77,11 @@ def tile_attend_sigm_cap_kb_segb2q128n512t2048_kernel(tc, q_words, q_scales, k_w
         nc.gpsimd.memset(qs[:].bitcast(I32), 0)
         qs_rows = q_scales.bitcast(I32).rearrange("b o (h r) q -> r h (b o) q", r=4)
         for r in range(4):
-            nc.sync.dma_start(qs[r:P:32, :].bitcast(I32).rearrange("h (c q) -> h c q", c=B * PASSES), qs_rows[r])
-        nc.gpsimd.memset(ks_pool[32:64, :].bitcast(I32), 0)
-        nc.gpsimd.memset(ks_pool[64:128, :].bitcast(I32), 0)
-        kb_pool = al.tile([P, T], F32, name="kb_pool", offset=0, align_bytes=64)
+            nc.sync.dma_start(qs[r:P:QUAD, :].bitcast(I32).rearrange("h (c q) -> h c q", c=B * PASSES), qs_rows[r])
+
+        nc.gpsimd.memset(ks_pool[QUAD : 2 * QUAD, :].bitcast(I32), 0)
+        nc.gpsimd.memset(ks_pool[2 * QUAD : P, :].bitcast(I32), 0)
+        kb_pool = al.tile([P, T], F32, name="kb_pool", offset=AT_KB_POOL, align_bytes=64)
         nc.gpsimd.memset(kb_pool[:].bitcast(I32), 0)
         nc.scalar.dma_start(kb_pool[0:1, :], kb[0:1, :])
         ident_bf = sb.tile([P, P], BF16, name="ident_bf", align_bytes=64)
@@ -74,100 +90,67 @@ def tile_attend_sigm_cap_kb_segb2q128n512t2048_kernel(tc, q_words, q_scales, k_w
         nc.gpsimd.memset(ks1[:].bitcast(I32), 0)
         make_identity(nc, ident_bf[:])
         make_identity(nc, ident[:])
-        vs_pool = al.tile([P, T], F32, name="vs_pool", offset=16384, align_bytes=64)
-        nc.gpsimd.memset(vs_pool[:].bitcast(I32), 0)
 
-        ks_got = sb.tile([P, B * N], U8, name="ks_got", align_bytes=64)
+        ks_got = al.tile([P, B * N], U8, name="ks_got", offset=AT_KS_GOT, align_bytes=64)
         for b in range(B):
             nc.vector.tensor_copy(ks_got[:, b * N : (b + 1) * N], listed(ks_pool[:], b))
-        qw = al.tile([P, B * PASSES, NQ], I32, name="qw", offset=12288, align_bytes=64)
+        qw = al.tile([P, B * PASSES, NQ], I32, name="qw", offset=AT_QW, align_bytes=64)
         nc.sync.dma_start(qw[:], q_words.rearrange("b o g q r -> g (b o) (q r)").bitcast(I32))
         ks0 = sb.tile([P, B * N], U8, name="ks0", align_bytes=64)
         ks_planes = [ks0, ks1]
-
-        def deal_key_scales():
-            for b in range(B):
-                nc.vector.tensor_copy(
-                    ks0[:, b * N : (b + 1) * N].bitcast(I32).rearrange("p (t m) -> p t m", t=PACK),
-                    ks_got[:, b * N : (b + 1) * N].bitcast(I32).rearrange("p (m t) -> p t m", t=PACK),
-                )
-            for o in range(PASSES):
-                for h in range(4):
-                    if (o, h) != (0, 0):
-                        row = 16 * o + 4 * h
-                        nc.sync.dma_start(ks_planes[o][32 * h : 32 * h + 4, :].bitcast(I32), ks0[row : row + 4, :].bitcast(I32))
-
-        v_pool = al.tile([P, T], BF16, name="v_pool", offset=28672, align_bytes=64)
-
-
-        def keys(b):
-            got = al.tile([P, N], U32, name=f"kw_got{b}", offset=(24576, 0)[b], align_bytes=64)
-            nc.vector.tensor_copy(dealt(got[:]), listed(kw_pool[:, 0 : (b + 1) * SEG].bitcast(U32), b))
-            return got
-
-        def part(got, b):
-            parted = al.tile([P, PASSES * N * 2], U8, name=f"kw_part{b}", offset=(2048, 26624)[b], align_bytes=64)
+        v_pool = al.tile([P, T], BF16, name="v_pool", offset=AT_V_POOL, align_bytes=64)
+        for b in range(B):
             nc.vector.tensor_copy(
-                parted[:].bitcast(U16).rearrange("p (o x) -> p o x", o=PASSES),
-                got[:].bitcast(U16).rearrange("p (x o) -> p o x", o=PASSES),
+                ks0[:, b * N : (b + 1) * N].bitcast(I32).rearrange("p (t m) -> p t m", t=PACK),
+                ks_got[:, b * N : (b + 1) * N].bitcast(I32).rearrange("p (m t) -> p t m", t=PACK),
             )
-            return parted
+        for o, h in [(o, h) for o in range(PASSES) for h in range(4)][1:]:
+            row = 16 * o + 4 * h
+            nc.sync.dma_start(ks_planes[o][QUAD * h : QUAD * h + 4, :].bitcast(I32), ks0[row : row + 4, :].bitcast(I32))
+        vs_pool = al.tile([P, T], F32, name="vs_pool", offset=AT_VS_POOL, align_bytes=64)
+        nc.gpsimd.memset(vs_pool[:].bitcast(I32), 0)
+        nc.sync.dma_start(vs_pool[0:1, :], vs[0:1, :])
 
-        def gather_biases():
-            got = sb.tile([P, B * N], U32, name="kb_got", align_bytes=64)
-            nc.vector.tensor_copy(dealt(got[:]), kb_pool[:].bitcast(U32).indirect(offsets[:]))
-            return got
-
-        def half_bias(got, b):
-            turned = ps.tile([P, PACK, P], F32, name=f"kb_turn{b}", tag=f"turn{b}")
-            for t in range(PACK):
-                first = (t * B + b) * P
-                nc.tensor.transpose(turned[:, t, :], got[:, first : first + P].bitcast(F32), ident[:])
-            half = al.tile([P, PACK], F32, name=f"kb_half{b}", offset=30720 + 64 * b, align_bytes=64)
-            nc.scalar.activation(half[:], turned[:, :, 0], ACT.Copy, scale=1.0 / CAP)
-            return half
-
-        def token_scale(b):
-            got = sb.tile([P, N], U32, name=f"vs_got{b}", align_bytes=64)
-            nc.vector.tensor_copy(dealt(got[:]), listed(vs_pool[:].bitcast(U32), b))
-            turned = ps.tile([P, PACK, P], F32, name=f"vs_turn{b}", tag=f"bank{b}_0")
-            for t in range(PACK):
-                nc.tensor.transpose(turned[:, t, :], got[:, t * P : (t + 1) * P].bitcast(F32), ident[:])
-            return turned[:, :, 0:1].rearrange("p t o -> p o t")
-
-        def values(b, pieces, scalar_cols):
+        def gather_values(b, pieces):
             width = SEG // pieces
             for h in range(pieces):
                 nc.scalar.copy(v_pool[:, b * SEG + h * width : b * SEG + (h + 1) * width], v_raw[b][:, h * width : (h + 1) * width])
-            got = sb.tile([P, N], BF16, name=f"v_got{b}", align_bytes=64)
-            first = b * COLS
-            nc.scalar.activation(
-                dealt(got[:])[:, 0:scalar_cols],
-                v_pool[:, 0 : (b + 1) * SEG].indirect(offsets[:, first : first + scalar_cols]),
-                ACT.Copy,
-            )
-            if scalar_cols < COLS:
-                nc.vector.tensor_copy(
-                    dealt(got[:])[:, scalar_cols:COLS],
-                    v_raw[b][:].indirect(offsets[:, first + scalar_cols : first + COLS]),
-                )
-            return got
+            v_got = sb.tile([P, N], BF16, name=f"v_got{b}", align_bytes=64)
+            nc.scalar.activation(dealt(v_got[:]), listed(v_pool[:, 0 : (b + 1) * SEG], b), ACT.Copy)
+            return v_got
 
-        def turn_values(got, b, tags):
-            woven = al.tile([P, DV, PACK], BF16, name=f"v_woven{b}", offset=(31744, 18432)[b], align_bytes=64)
-            places = PACK // len(tags)
-            for h, tag in enumerate(tags):
-                turned = ps.tile([P, places, P], BF16, name=f"v_turn{b}_{h}", tag=tag)
-                for j in range(places):
-                    t = h * places + j
-                    nc.tensor.transpose(turned[:, j, :], got[:, t * P : (t + 1) * P], ident_bf[:])
-                (nc.scalar.copy, nc.vector.tensor_copy)[b](woven[:, :, h * places : (h + 1) * places], turned[:].rearrange("p t e -> p e t"))
+        def gather_keys(b):
+            kw_got = al.tile([P, N], U32, name=f"kw_got{b}", offset=AT_KW_GOT[b], align_bytes=64)
+            nc.vector.tensor_copy(dealt(kw_got[:]), listed(kw_pool[:, 0 : (b + 1) * SEG].bitcast(U32), b))
+            return kw_got
+
+        def part_keys(kw_got, b):
+            parted = al.tile([P, PASSES * N * 2], U8, name=f"kw_part{b}", offset=AT_KW_PART[b], align_bytes=64)
+            nc.vector.tensor_copy(
+                parted[:].bitcast(U16).rearrange("p (o x) -> p o x", o=PASSES),
+                kw_got[:].bitcast(U16).rearrange("p (x o) -> p o x", o=PASSES),
+            )
+            return parted
+
+        def turn_bias(kb_got, b):
+            turned = ps.tile([P, PACK, P], F32, name=f"kb_turn{b}", tag=f"turn{b}")
+            for t in range(PACK):
+                first = (t * B + b) * P
+                nc.tensor.transpose(turned[:, t, :], kb_got[:, first : first + P].bitcast(F32), ident[:])
+            bias = sb.tile([P, PACK], F32, name=f"kb_half{b}")
+            nc.vector.tensor_scalar(bias[:], turned[:, :, 0], 1.0 / CAP, None, ALU.mult)
+            return bias
+
+        def turn_values(v_got, b, tag, copy):
+            woven = al.tile([P, DV, PACK], BF16, name=f"v_woven{b}", offset=AT_WOVEN[b], align_bytes=64)
+            turned = ps.tile([P, PACK, P], BF16, name=f"v_turn{b}_0", tag=tag)
+            for t in range(PACK):
+                nc.tensor.transpose(turned[:, t, :], v_got[:, t * P : (t + 1) * P], ident_bf[:])
+            copy(woven[:], turned[:].rearrange("p t e -> p e t"))
             return woven
 
-        def weights(b, parted, bias):
-            banks = [
-                ps.tile([P, 2, NQ], F32, name=f"scores{b}_{h}", tag=f"bank{b}_{h}") for h in range(2)
-            ]
+        def probabilities(b, parted, bias):
+            banks = [ps.tile([P, 2, NQ], F32, name=f"scores{b}_{h}", tag=f"bank{b}_{h}") for h in range(2)]
             scores = [banks[t // 2][:, t % 2, :] for t in range(PACK)]
             for t in range(PACK):
                 for o in range(PASSES):
@@ -181,66 +164,69 @@ def tile_attend_sigm_cap_kb_segb2q128n512t2048_kernel(tc, q_words, q_scales, k_w
                         start=(o == 0),
                         stop=(o == PASSES - 1),
                     )
-            capped = al.tile([P, PACK, NQ], F32, name=f"capped{b}", offset=(28672, 32768)[b], align_bytes=64)
+            capped = al.tile([P, PACK, NQ], F32, name=f"capped{b}", offset=AT_CAPPED[b], align_bytes=64)
             for t in range(PACK):
                 nc.scalar.activation(capped[:, t, :], scores[t], ACT.Tanh, bias=bias[:, t : t + 1], scale=1.0 / CAP)
-            return capped
-
-        def sigmoid(capped, b):
             prob = sb.tile([P, NQ, PACK], F32, name=f"prob{b}", align_bytes=64)
             nc.scalar.activation(prob[:], capped[:].rearrange("p t q -> p q t"), ACT.Sigmoid, scale=CAP)
             return prob
 
-        def quantise(src, name):
-            codes = sb.tile([P, P], U32, name=name + "_codes", align_bytes=64)
-            scales = sb.tile([P, P], U8, name=name + "_scales", align_bytes=64)
-            nc.vector.quantize_mx(codes[:].bitcast(FP8X4), scales[:], src)
-            return codes, scales
+        def token_scale(b):
+            vs_got = sb.tile([P, N], U32, name=f"vs_got{b}", align_bytes=64)
+            nc.vector.tensor_copy(dealt(vs_got[:]), listed(vs_pool[:].bitcast(U32), b))
+            turned = ps.tile([P, PACK, P], F32, name=f"vs_turn{b}", tag=f"bank{b}_0")
+            for t in range(PACK):
+                nc.tensor.transpose(turned[:, t, :], vs_got[:, t * P : (t + 1) * P].bitcast(F32), ident[:])
+            return turned[:, :, 0:1].rearrange("p t o -> p o t")
 
-        deal_key_scales()
-        nc.sync.dma_start(vs_pool[0:1, :], vs[0:1, :])
-        v_got0 = values(0, 2, COLS)
-        v_got1 = values(1, 1, COLS)
-        got0 = keys(0)
-        kb_got = gather_biases()
-        parted0 = part(got0, 0)
-        parted1 = part(keys(1), 1)
-        v_codes = al.tile([P, B * DV], U32, name="v_codes", offset=16384, align_bytes=64)
+        v_got0 = gather_values(0, pieces=2)
+        v_got1 = gather_values(1, pieces=1)
+        kw_got0 = gather_keys(0)
+        kb_got = sb.tile([P, B * N], U32, name="kb_got", align_bytes=64)
+        nc.vector.tensor_copy(dealt(kb_got[:]), kb_pool[:].bitcast(U32).indirect(offsets[:]))
+        parted0 = part_keys(kw_got0, 0)
+        parted1 = part_keys(gather_keys(1), 1)
+        v_codes = al.tile([P, B * DV], U32, name="v_codes", offset=AT_V_CODES, align_bytes=64)
         v_scales = sb.tile([P, B * DV], U8, name="v_scales", align_bytes=64)
 
         def quantise_values(woven, b):
             cols = slice(b * DV, (b + 1) * DV)
             nc.vector.quantize_mx(v_codes[:, cols].bitcast(FP8X4), v_scales[:, cols], woven[:].rearrange("p e t -> p (e t)"))
 
-        bias0 = half_bias(kb_got, 0)
-        bias1 = half_bias(kb_got, 1)
-        woven0 = turn_values(v_got0, 0, ("values0",))
-        prob0 = sigmoid(weights(0, parted0, bias0), 0)
-        prob1 = sigmoid(weights(1, parted1, bias1), 1)
+        bias0 = turn_bias(kb_got, 0)
+        bias1 = turn_bias(kb_got, 1)
+        woven0 = turn_values(v_got0, 0, "values0", nc.scalar.copy)
+        prob0 = probabilities(0, parted0, bias0)
+        prob1 = probabilities(1, parted1, bias1)
         scale0 = token_scale(0)
         scale1 = token_scale(1)
-        woven1 = turn_values(v_got1, 1, ("bank0_1",))
-        wq = []
-        w_bf = []
+        woven1 = turn_values(v_got1, 1, "bank0_1", nc.vector.tensor_copy)
+
+        weights = []
         for b, (prob, scale) in enumerate(((prob0, scale0), (prob1, scale1))):
             w = sb.tile([P, NQ, PACK], BF16, name=f"w{b}", align_bytes=64)
             nc.vector.tensor_tensor(w[:], prob[:], scale.to_broadcast([P, NQ, PACK]), ALU.mult)
-            w_bf.append(w)
+            weights.append(w)
         quantise_values(woven0, 0)
+        w_mx = []
         for b in range(B):
-            wq.append(quantise(w_bf[b][:].rearrange("p q t -> p (q t)"), f"wq{b}"))
+            w_codes = sb.tile([P, NQ], U32, name=f"wq{b}_codes", align_bytes=64)
+            w_scales = sb.tile([P, NQ], U8, name=f"wq{b}_scales", align_bytes=64)
+            nc.vector.quantize_mx(w_codes[:].bitcast(FP8X4), w_scales[:], weights[b][:].rearrange("p q t -> p (q t)"))
+            w_mx.append((w_codes, w_scales))
         quantise_values(woven1, 1)
-        for b in range(B):
+
+        for b, (w_codes, w_scales) in enumerate(w_mx):
             y = ps.tile([P, DV], F32, name=f"y{b}", tag=f"turn{b}")
             nc.tensor.matmul_mx(
                 y[:],
-                lhsT=wq[b][0][:].bitcast(FP8X4),
-                lhsT_scale=wq[b][1][:],
+                lhsT=w_codes[:].bitcast(FP8X4),
+                lhsT_scale=w_scales[:],
                 rhs=v_codes[:, b * DV : (b + 1) * DV].bitcast(FP8X4),
                 rhs_scale=v_scales[:, b * DV : (b + 1) * DV],
                 start=True,
                 stop=True,
             )
             res = sb.tile([P, DV], F32, name=f"res{b}")
-            nc.scalar.activation(res[:], y[:], ACT.Copy, scale=1.0 / 16.0)
+            nc.scalar.activation(res[:], y[:], ACT.Copy, scale=OUT_SCALE)
             nc.sync.dma_start(out[b], res[:])

from contextlib import ExitStack

import concourse.mybir as mybir
from concourse.masks import make_identity

B, N, T, D, DV, NQ = 2, 512, 2048, 1024, 128, 128
P = 128
PACK = 4
PASSES = D // (P * PACK)
SEG = T // B
COLS = N // 16
RUN = 4
QUAD = 32
CAP = 2.0
OUT_SCALE = 1.0 / 16.0

FLOPS = 2 * B * NQ * N * (D + DV)

F32 = mybir.dt.float32
BF16 = mybir.dt.bfloat16
I32 = mybir.dt.int32
U32 = mybir.dt.uint32
U16 = mybir.dt.uint16
U8 = mybir.dt.uint8
FP8X4 = mybir.dt.float8_e4m3fn_x4
FP4X4 = mybir.dt.float4_e2m1fn_x4
ACT = mybir.ActivationFunctionType
ALU = mybir.AluOpType

KIB = 1024
AT_KB_POOL = 0
AT_KW_GOT = (24 * KIB, AT_KB_POOL)
AT_KW_PART = (AT_KB_POOL + 2 * KIB, 26 * KIB)
AT_KS_POOL = 11 * KIB
AT_QW = AT_KS_POOL + KIB
AT_VS_POOL = 16 * KIB
AT_KS_GOT = AT_VS_POOL
AT_V_CODES = AT_VS_POOL
AT_V_POOL = 28 * KIB
AT_CAPPED = (AT_V_POOL, 32 * KIB)
AT_WOVEN = (AT_V_POOL + 3 * KIB, AT_VS_POOL + 2 * KIB)


def tile_attend_sigm_cap_kb_segb2q128n512t2048_kernel(tc, q_words, q_scales, k_words, k_scales, vT, vs, kb, offs, out):
    nc = tc.nc
    with ExitStack() as ctx:
        sb = ctx.enter_context(tc.tile_pool(name="sb", bufs=1))
        al = ctx.enter_context(tc.tile_pool(name="al", bufs=1))
        ps = ctx.enter_context(tc.psum_pool(name="ps", bufs=1))

        offsets = sb.tile([P, B * COLS], U16, name="offsets")
        nc.sync.dma_start(offsets[:], offs)

        def dealt(tile_ap):
            return tile_ap.rearrange("p (t m i) -> p m t i", t=PACK, i=RUN)

        def listed(window, b):
            return window.indirect(offsets[:, b * COLS : (b + 1) * COLS])

        warm_in = sb.tile([P, 1], F32, name="warm_in")
        nc.vector.memset(warm_in[:], 0.0)
        warm = sb.tile([P, 1], F32, name="warm")
        nc.scalar.activation(warm[:], warm_in[:], ACT.Sigmoid)

        ks_pool = al.tile([P, T], U8, name="ks_pool", offset=AT_KS_POOL, align_bytes=64)
        nc.sync.dma_start(ks_pool[0:QUAD, :].bitcast(I32), k_scales.bitcast(I32).rearrange("o f t -> (o f) t"))
        kw_pool = sb.tile([P, T], I32, name="kw_pool", align_bytes=64)
        kw_dram = k_words[0].rearrange("g t x -> g (t x)").bitcast(I32)
        v_raw = [sb.tile([P, SEG], F32, name=f"v_raw{b}", align_bytes=64) for b in range(B)]
        for h in range(2):
            nc.sync.dma_start(v_raw[0][:, h * SEG // 2 : (h + 1) * SEG // 2], vT[:, h * SEG // 2 : (h + 1) * SEG // 2])
        nc.sync.dma_start(kw_pool[:, 0:SEG], kw_dram[:, 0:SEG])
        nc.sync.dma_start(v_raw[1][:], vT[:, SEG:T])
        nc.sync.dma_start(kw_pool[:, SEG:T], kw_dram[:, SEG:T])

        qs = sb.tile([P, B * PASSES * NQ], U8, name="qs", align_bytes=64)
        nc.gpsimd.memset(qs[:].bitcast(I32), 0)
        qs_rows = q_scales.bitcast(I32).rearrange("b o (h r) q -> r h (b o) q", r=4)
        for r in range(4):
            nc.sync.dma_start(qs[r:P:QUAD, :].bitcast(I32).rearrange("h (c q) -> h c q", c=B * PASSES), qs_rows[r])

        nc.gpsimd.memset(ks_pool[QUAD : 2 * QUAD, :].bitcast(I32), 0)
        nc.gpsimd.memset(ks_pool[2 * QUAD : P, :].bitcast(I32), 0)
        kb_pool = al.tile([P, T], F32, name="kb_pool", offset=AT_KB_POOL, align_bytes=64)
        nc.gpsimd.memset(kb_pool[:].bitcast(I32), 0)
        nc.scalar.dma_start(kb_pool[0:1, :], kb[0:1, :])
        ident_bf = sb.tile([P, P], BF16, name="ident_bf", align_bytes=64)
        ident = sb.tile([P, P], F32, name="ident", align_bytes=64)
        ks1 = sb.tile([P, B * N], U8, name="ks1", align_bytes=64)
        nc.gpsimd.memset(ks1[:].bitcast(I32), 0)
        make_identity(nc, ident_bf[:])
        make_identity(nc, ident[:])

        ks_got = al.tile([P, B * N], U8, name="ks_got", offset=AT_KS_GOT, align_bytes=64)
        for b in range(B):
            nc.vector.tensor_copy(ks_got[:, b * N : (b + 1) * N], listed(ks_pool[:], b))
        qw = al.tile([P, B * PASSES, NQ], I32, name="qw", offset=AT_QW, align_bytes=64)
        nc.sync.dma_start(qw[:], q_words.rearrange("b o g q r -> g (b o) (q r)").bitcast(I32))
        ks0 = sb.tile([P, B * N], U8, name="ks0", align_bytes=64)
        ks_planes = [ks0, ks1]
        v_pool = al.tile([P, T], BF16, name="v_pool", offset=AT_V_POOL, align_bytes=64)
        for b in range(B):
            nc.vector.tensor_copy(
                ks0[:, b * N : (b + 1) * N].bitcast(I32).rearrange("p (t m) -> p t m", t=PACK),
                ks_got[:, b * N : (b + 1) * N].bitcast(I32).rearrange("p (m t) -> p t m", t=PACK),
            )
        for o, h in [(o, h) for o in range(PASSES) for h in range(4)][1:]:
            row = 16 * o + 4 * h
            nc.sync.dma_start(ks_planes[o][QUAD * h : QUAD * h + 4, :].bitcast(I32), ks0[row : row + 4, :].bitcast(I32))
        vs_pool = al.tile([P, T], F32, name="vs_pool", offset=AT_VS_POOL, align_bytes=64)
        nc.gpsimd.memset(vs_pool[:].bitcast(I32), 0)
        nc.sync.dma_start(vs_pool[0:1, :], vs[0:1, :])

        def gather_values(b, pieces):
            width = SEG // pieces
            for h in range(pieces):
                nc.scalar.copy(v_pool[:, b * SEG + h * width : b * SEG + (h + 1) * width], v_raw[b][:, h * width : (h + 1) * width])
            v_got = sb.tile([P, N], BF16, name=f"v_got{b}", align_bytes=64)
            nc.scalar.activation(dealt(v_got[:]), listed(v_pool[:, 0 : (b + 1) * SEG], b), ACT.Copy)
            return v_got

        def gather_keys(b):
            kw_got = al.tile([P, N], U32, name=f"kw_got{b}", offset=AT_KW_GOT[b], align_bytes=64)
            nc.vector.tensor_copy(dealt(kw_got[:]), listed(kw_pool[:, 0 : (b + 1) * SEG].bitcast(U32), b))
            return kw_got

        def part_keys(kw_got, b):
            parted = al.tile([P, PASSES * N * 2], U8, name=f"kw_part{b}", offset=AT_KW_PART[b], align_bytes=64)
            nc.vector.tensor_copy(
                parted[:].bitcast(U16).rearrange("p (o x) -> p o x", o=PASSES),
                kw_got[:].bitcast(U16).rearrange("p (x o) -> p o x", o=PASSES),
            )
            return parted

        def turn_bias(kb_got, b):
            turned = ps.tile([P, PACK, P], F32, name=f"kb_turn{b}", tag=f"turn{b}")
            for t in range(PACK):
                first = (t * B + b) * P
                nc.tensor.transpose(turned[:, t, :], kb_got[:, first : first + P].bitcast(F32), ident[:])
            bias = sb.tile([P, PACK], F32, name=f"kb_half{b}")
            nc.vector.tensor_scalar(bias[:], turned[:, :, 0], 1.0 / CAP, None, ALU.mult)
            return bias

        def turn_values(v_got, b, tag, copy):
            woven = al.tile([P, DV, PACK], BF16, name=f"v_woven{b}", offset=AT_WOVEN[b], align_bytes=64)
            turned = ps.tile([P, PACK, P], BF16, name=f"v_turn{b}_0", tag=tag)
            for t in range(PACK):
                nc.tensor.transpose(turned[:, t, :], v_got[:, t * P : (t + 1) * P], ident_bf[:])
            copy(woven[:], turned[:].rearrange("p t e -> p e t"))
            return woven

        def probabilities(b, parted, bias):
            banks = [ps.tile([P, 2, NQ], F32, name=f"scores{b}_{h}", tag=f"bank{b}_{h}") for h in range(2)]
            scores = [banks[t // 2][:, t % 2, :] for t in range(PACK)]
            for t in range(PACK):
                for o in range(PASSES):
                    c = b * PASSES + o
                    nc.tensor.matmul_mx(
                        scores[t],
                        lhsT=parted[:, (o * PACK + t) * 2 * P : (o * PACK + t + 1) * 2 * P].bitcast(FP4X4),
                        lhsT_scale=ks_planes[o][:, b * N + t * P : b * N + (t + 1) * P],
                        rhs=qw[:, c, :].bitcast(FP8X4),
                        rhs_scale=qs[:, c * NQ : (c + 1) * NQ],
                        start=(o == 0),
                        stop=(o == PASSES - 1),
                    )
            capped = al.tile([P, PACK, NQ], F32, name=f"capped{b}", offset=AT_CAPPED[b], align_bytes=64)
            for t in range(PACK):
                nc.scalar.activation(capped[:, t, :], scores[t], ACT.Tanh, bias=bias[:, t : t + 1], scale=1.0 / CAP)
            prob = sb.tile([P, NQ, PACK], F32, name=f"prob{b}", align_bytes=64)
            nc.scalar.activation(prob[:], capped[:].rearrange("p t q -> p q t"), ACT.Sigmoid, scale=CAP)
            return prob

        def token_scale(b):
            vs_got = sb.tile([P, N], U32, name=f"vs_got{b}", align_bytes=64)
            nc.vector.tensor_copy(dealt(vs_got[:]), listed(vs_pool[:].bitcast(U32), b))
            turned = ps.tile([P, PACK, P], F32, name=f"vs_turn{b}", tag=f"bank{b}_0")
            for t in range(PACK):
                nc.tensor.transpose(turned[:, t, :], vs_got[:, t * P : (t + 1) * P].bitcast(F32), ident[:])
            return turned[:, :, 0:1].rearrange("p t o -> p o t")

        v_got0 = gather_values(0, pieces=2)
        v_got1 = gather_values(1, pieces=1)
        kw_got0 = gather_keys(0)
        kb_got = sb.tile([P, B * N], U32, name="kb_got", align_bytes=64)
        nc.vector.tensor_copy(dealt(kb_got[:]), kb_pool[:].bitcast(U32).indirect(offsets[:]))
        parted0 = part_keys(kw_got0, 0)
        parted1 = part_keys(gather_keys(1), 1)
        v_codes = al.tile([P, B * DV], U32, name="v_codes", offset=AT_V_CODES, align_bytes=64)
        v_scales = sb.tile([P, B * DV], U8, name="v_scales", align_bytes=64)

        def quantise_values(woven, b):
            cols = slice(b * DV, (b + 1) * DV)
            nc.vector.quantize_mx(v_codes[:, cols].bitcast(FP8X4), v_scales[:, cols], woven[:].rearrange("p e t -> p (e t)"))

        bias0 = turn_bias(kb_got, 0)
        bias1 = turn_bias(kb_got, 1)
        woven0 = turn_values(v_got0, 0, "values0", nc.scalar.copy)
        prob0 = probabilities(0, parted0, bias0)
        prob1 = probabilities(1, parted1, bias1)
        scale0 = token_scale(0)
        scale1 = token_scale(1)
        woven1 = turn_values(v_got1, 1, "bank0_1", nc.vector.tensor_copy)

        weights = []
        for b, (prob, scale) in enumerate(((prob0, scale0), (prob1, scale1))):
            w = sb.tile([P, NQ, PACK], BF16, name=f"w{b}", align_bytes=64)
            nc.vector.tensor_tensor(w[:], prob[:], scale.to_broadcast([P, NQ, PACK]), ALU.mult)
            weights.append(w)
        quantise_values(woven0, 0)
        w_mx = []
        for b in range(B):
            w_codes = sb.tile([P, NQ], U32, name=f"wq{b}_codes", align_bytes=64)
            w_scales = sb.tile([P, NQ], U8, name=f"wq{b}_scales", align_bytes=64)
            nc.vector.quantize_mx(w_codes[:].bitcast(FP8X4), w_scales[:], weights[b][:].rearrange("p q t -> p (q t)"))
            w_mx.append((w_codes, w_scales))
        quantise_values(woven1, 1)

        for b, (w_codes, w_scales) in enumerate(w_mx):
            y = ps.tile([P, DV], F32, name=f"y{b}", tag=f"turn{b}")
            nc.tensor.matmul_mx(
                y[:],
                lhsT=w_codes[:].bitcast(FP8X4),
                lhsT_scale=w_scales[:],
                rhs=v_codes[:, b * DV : (b + 1) * DV].bitcast(FP8X4),
                rhs_scale=v_scales[:, b * DV : (b + 1) * DV],
                start=True,
                stop=True,
            )
            res = sb.tile([P, DV], F32, name=f"res{b}")
            nc.scalar.activation(res[:], y[:], ACT.Copy, scale=OUT_SCALE)
            nc.sync.dma_start(out[b], res[:])
